import numpy as np
import ml_dtypes


def mxq(x, axis, fmt="e4m3"):
    dtype, down = {"e4m3": (ml_dtypes.float8_e4m3fn, 7), "e5m2": (ml_dtypes.float8_e5m2, 14)}[fmt]
    v = np.moveaxis(np.asarray(x, np.float32).astype(ml_dtypes.bfloat16).astype(np.float64), axis, -1)
    blocks = v.reshape(v.shape[:-1] + (-1, 32))
    amax = np.abs(blocks).max(-1, keepdims=True)
    byte = np.maximum(np.where(amax > 0, np.frexp(amax)[1] - 1 + 127, 0) - down, 1)
    scale = np.exp2(byte - 127.0)
    codes = (blocks / scale).astype(np.float32).astype(dtype).astype(np.float64)
    return np.moveaxis((codes * scale).reshape(v.shape), -1, axis)


WIDE = False


def mx_kscale(k):
    if not WIDE:
        return np.ones(k)
    levels = np.array([10, -10, 5, -5, 0])
    if k % 512:
        return np.exp2(np.random.permutation(np.resize(levels, k // 32))).repeat(32)
    a = np.empty((k // 512, 16))
    for p in range(k // 512):
        a[p, :8] = np.random.permutation(np.resize(levels, 8))
        for g in range(8):
            far = levels[np.abs(levels - a[p, g]) >= 10]
            a[p, g + 8] = far[np.random.randint(len(far))]
    return np.exp2(a.ravel()).repeat(32)


def f64(x):
    return np.asarray(x).astype(np.float64)


def striped(idx):
    return np.tile(idx.reshape(-1, 16).T, (8, 1)).astype(np.uint16)


def unstriped(offs):
    return offs[:16].T.reshape(-1).astype(np.int64)


def striped8(idx):
    return np.concatenate([x.reshape(-1, 16).T for x in idx]).astype(np.uint16)


def runs(offs, k):
    lists = np.stack([offs[16 * r : 16 * r + 16].T.reshape(-1) for r in range(8)]).astype(np.int64)
    return lists[np.arange(k) % 512 // 64]


def pack_weight(w):
    k, n = w.shape
    w = f64(np.asarray(w, np.float32).astype(ml_dtypes.bfloat16)).reshape(k // 32, 32, n)
    amax = np.abs(w).max(1)
    byte = np.clip(np.where(amax > 0, np.frexp(amax)[1] - 1 + 127 - 7, 1), 1, 254)
    scaled = (w * np.exp2(127.0 - byte)[:, None, :]).reshape(k, n).astype(np.float32)
    words = np.ascontiguousarray(scaled.reshape(k // 512, 128, 4, n).transpose(0, 1, 3, 2)).astype(ml_dtypes.float8_e4m3fn).view(np.uint8)
    return words, np.ascontiguousarray(byte.astype(np.uint8).reshape(k // 512, 16, n))


def unpack_weight(words, scales):
    g, p, n, _ = words.shape
    vals = np.ascontiguousarray(words).view(ml_dtypes.float8_e4m3fn).astype(np.float64) * np.repeat(np.exp2(scales.astype(np.float64) - 127.0), 8, axis=1)[..., None]
    return vals.transpose(0, 1, 3, 2).reshape(g * 512, n)


K, T, S, H, C, G, W = 512, 1024, 512, 512, 512, 2048, 256


def setup_inputs():
    n = np.random.standard_normal
    s = mx_kscale(K)[:, None]
    packed_xT = pack_weight(n((K, T)) * s)
    packed_dT = pack_weight(n((K, G)) / s)
    return {
        "x_words": packed_xT[0],
        "x_scales": packed_xT[1],
        "w1": (n((K, H)) / np.sqrt(K) / s).astype(np.float32),
        "gs": (np.random.uniform(0.5, 1.5, (K, 1)) / s).astype(np.float32),
        "gk": (np.random.uniform(0.5, 1.5, (K, 1)) * s).astype(np.float32),
        "d_words": packed_dT[0],
        "d_scales": packed_dT[1],
        "offs": striped(np.random.permutation(T)[:S]),
        "n1": striped8(np.stack([np.random.permutation(S) for _ in range(8)])),
        "n2": striped8(np.stack([np.random.permutation(S) for _ in range(8)])),
        "n3": striped(np.random.permutation(S)),
        "n4": striped(np.random.permutation(S)),
        "cand": striped(np.random.permutation(T)[:C]),
        "k1": striped8(np.random.randint(0, G, (8, H))),
        "n5": striped(np.random.permutation(S)[:W]),
        "n6": striped(np.random.permutation(S)[:W]),
    }


def reference(x_words, x_scales, w1, gs, gk, d_words, d_scales, offs, n1, n2, n3, n4, cand, k1, n5, n6):
    d_k1 = unpack_weight(d_words, d_scales)[np.arange(K)[:, None], runs(k1, K)]
    xq = unpack_weight(x_words, x_scales)[:, unstriped(offs)]
    y = mxq(f64(w1), 0, "e4m3").T @ xq
    z2 = f64(gk) * (y[:, unstriped(n3)] + 0.75 * y[:, unstriped(n4)])
    b = 0.0625 * ((d_k1.T @ mxq(z2, 0, "e4m3")))
    x_cand = unpack_weight(x_words, x_scales)[:, unstriped(cand)]
    z = f64(gs) * (0.75 * ((y - (y[np.arange(H)[:, None], runs(n1, H)])) * (y - (y[np.arange(H)[:, None], runs(n2, H)]))))
    a = 0.0625 * ((x_cand.T @ mxq(z, 0, "e4m3")))
    ra = b[:, unstriped(n6)] - (0.5 * a[:, unstriped(n5)])
    out = a.copy()
    out[:, unstriped(n5)] = ra
    return out

@@ -1,0 +1,212 @@
+from contextlib import ExitStack
+
+import concourse.mybir as mybir
+
+K, T, S, H, C, G, W = 512, 1024, 512, 512, 512, 2048, 256
+FLOPS = 3 * 2 * 512 * 512 * 512
+
+F32 = mybir.dt.float32
+BF16 = mybir.dt.bfloat16
+I32 = mybir.dt.int32
+U32 = mybir.dt.uint32
+U16 = mybir.dt.uint16
+U8 = mybir.dt.uint8
+FP8X4 = mybir.dt.float8_e4m3fn_x4
+MULT = mybir.AluOpType.mult
+ADD = mybir.AluOpType.add
+SUB = mybir.AluOpType.subtract
+COPY = mybir.ActivationFunctionType.Copy
+
+P = 128
+PACK = 4
+QUAD = 32
+
+
+def tile_picked_cdkeyputbquadsum_none_p_kernel(
+    tc, x_words, x_scales, w1, gs, gk, d_words, d_scales, offs, n1, n2, n3, n4, cand, k1, n5, n6, out
+):
+    nc = tc.nc
+    with ExitStack() as ctx:
+        keep = ctx.enter_context(tc.tile_pool(name="keep", bufs=1))
+        psum = ctx.enter_context(tc.psum_pool(name="psum", bufs=1))
+
+        def sb(name, shape, dtype, tag=None):
+            return keep.tile(shape, dtype, name=name, tag=tag or name, align_bytes=64)
+
+        def load_list(name, src):
+            tile = sb(name, list(src.shape), U16)
+            nc.sync.dma_start(tile[:], src)
+            return tile
+
+        x_tab_s = sb("x_tab_s", [P, T], U8)
+        d_tab_s = sb("d_tab_s", [P, G], U8)
+        key_s = sb("key_s", [P, H], U8)
+        nc.vector.memset(d_tab_s[:].bitcast(I32), 0)
+        nc.vector.memset(key_s[:].bitcast(I32), 0)
+        y_win = [sb("y_win%d" % t, [P, 2 * S], F32) for t in range(PACK)]
+        for t in range(PACK):
+            nc.vector.memset(y_win[t][:, S:], 0.0)
+
+        x_tab_w = sb("x_tab_w", [P, T], I32)
+        x_scale_rows = x_scales[0].bitcast(I32)
+        offs_l = load_list("offs_l", offs)
+        cand_l = load_list("cand_l", cand)
+        for q in range(P // QUAD):
+            rows = x_scale_rows[PACK * q : PACK * (q + 1), :].unsqueeze(0).to_broadcast([QUAD // PACK, PACK, T // 4])
+            nc.scalar.dma_start(x_tab_s[:].bitcast(I32)[QUAD * q : QUAD * (q + 1), :], rows)
+        halves = 2
+        HW = H // halves
+        w_raw = [sb("w_raw%d" % h, [P, PACK, HW], F32) for h in range(halves)]
+        w_rows = w1.rearrange("(p j) c -> p j c", j=PACK)
+        for h in range(halves):
+            nc.sync.dma_start(w_raw[h][:], w_rows[:, :, h * HW : (h + 1) * HW])
+            if h == 0:
+                nc.sync.dma_start(x_tab_w[:], x_words[0].rearrange("p n t -> p (n t)").bitcast(I32))
+        n1_l = load_list("n1_l", n1)
+        n2_l = load_list("n2_l", n2)
+        k1_l = load_list("k1_l", k1)
+        d_tab_w = sb("d_tab_w", [P, G], I32)
+        nc.sync.dma_start(d_tab_w[:], d_words[0].rearrange("p n t -> p (n t)").bitcast(I32))
+        nc.sync.dma_start(d_tab_s[:].bitcast(I32)[0:P:8, :], d_scales[0].bitcast(I32))
+        gs4 = sb("gs4", [P, PACK], F32)
+        gk4 = sb("gk4", [P, PACK], F32)
+        nc.sync.dma_start(gs4[:], gs.rearrange("(p t) o -> p (t o)", t=PACK))
+        nc.sync.dma_start(gk4[:], gk.rearrange("(p t) o -> p (t o)", t=PACK))
+        n4_l = load_list("n4_l", n4)
+        n3_l = load_list("n3_l", n3)
+        n5_l = load_list("n5_l", n5)
+        n6_l = load_list("n6_l", n6)
+
+        def gather_words(name, table, lst, tag=None):
+            words = sb(name, [P, 512], U32, tag)
+            nc.vector.tensor_copy(words[:], table[:].bitcast(U32).indirect(lst[:]))
+            return words
+
+        def gather_bytes(name, table, lst, tag=None):
+            scales = sb(name, [P, 512], U8, tag)
+            nc.vector.tensor_copy(scales[:], table[:].indirect(lst[:]))
+            return scales
+
+        tok_s = gather_bytes("tok_s", x_tab_s, offs_l)
+        cand_s = gather_bytes("cand_s", x_tab_s, cand_l)
+        tok_w = gather_words("tok_w", x_tab_w, offs_l)
+
+        MH = P // halves
+        w_bf = [sb("w_bf%d" % u, [P, 2, P, PACK], BF16) for u in range(2)]
+        w_q = [sb("w_q%d" % u, [P, 2 * P], U32) for u in range(2)]
+        w_s = [sb("w_s%d" % u, [P, 2 * P], U8) for u in range(2)]
+        for h in range(halves):
+            src = w_raw[h][:].rearrange("p j (m t) -> p m j t", t=PACK)
+            for u in range(2):
+                deal = nc.vector.tensor_copy if (h, u) == (1, 0) else nc.scalar.copy
+                deal(
+                    w_bf[u][:, :, h * MH : (h + 1) * MH, :].rearrange("p e m j -> p m j e"),
+                    src[:, :, :, 2 * u : 2 * u + 2],
+                )
+        for u in range(2):
+            nc.vector.quantize_mx(
+                out=w_q[u][:].bitcast(FP8X4), scales=w_s[u][:], in_=w_bf[u][:].rearrange("p e m j -> p (e m j)")
+            )
+
+        def product(tag, lhs_w, lhs_s, rhs_w, rhs_s):
+            bank = psum.tile([P, 512], F32, name=tag, tag=tag)
+            nc.tensor.matmul_mx(
+                out=bank[:], lhsT=lhs_w.bitcast(FP8X4), lhsT_scale=lhs_s, rhs=rhs_w.bitcast(FP8X4), rhs_scale=rhs_s,
+                start=True, stop=True,
+            )
+            return bank
+
+        y_ps = []
+        for t in range(PACK):
+            cols = slice((t % 2) * P, (t % 2 + 1) * P)
+            y_ps.append(product("yb%d" % t, w_q[t // 2][:, cols], w_s[t // 2][:, cols], tok_w[:], tok_s[:]))
+
+        cand_w = gather_words("cand_w", x_tab_w, cand_l, "w_bf1")
+
+        g1 = [sb("g1_%d" % t, [P, S], F32) for t in range(PACK)]
+        g2 = [sb("g2_%d" % t, [P, S], F32) for t in range(PACK)]
+        d1 = [sb("d1_%d" % t, [P, S], F32) for t in range(PACK)]
+        d2 = [sb("d2_%d" % t, [P, S], F32) for t in range(PACK)]
+        quad = sb("quad", [P, PACK, S], F32)
+        for t in range(PACK):
+            nc.scalar.copy(y_win[t][:, :S], y_ps[t][:])
+            nc.scalar.activation(g1[t][:], y_win[t][:].indirect(n1_l[:]), COPY)
+            if t == PACK - 1:
+                nc.vector.tensor_copy(g2[t][:], y_win[t][:].indirect(n2_l[:]))
+            else:
+                nc.scalar.activation(g2[t][:], y_win[t][:].indirect(n2_l[:]), COPY)
+            nc.vector.tensor_tensor(d1[t][:], g1[t][:], y_win[t][:, :S], SUB)
+            nc.vector.tensor_tensor(d2[t][:], g2[t][:], y_win[t][:, :S], SUB)
+            if t == 0:
+                key_gs = gather_bytes("key_gs", d_tab_s, k1_l)
+                key_w = gather_words("key_w", d_tab_w, k1_l)
+                for r in range(PACK):
+                    nc.sync.dma_start(key_s[:].bitcast(I32)[r:P:QUAD, :], key_gs[:].bitcast(I32)[8 * r : P : QUAD, :])
+            nc.vector.scalar_tensor_tensor(quad[:, t, :], d1[t][:], gs4[:, t : t + 1], d2[t][:], MULT, MULT)
+
+        g4 = [sb("g4_%d" % t, [P, S], F32) for t in range(PACK)]
+        for t in range(PACK):
+            nc.scalar.activation(g4[t][:], y_win[t][:].indirect(n4_l[:]), COPY, scale=0.75)
+
+        SH = S // 2
+        z_bf = [sb("z_bf%d" % h, [P, SH, PACK], BF16) for h in range(2)]
+        z_q = sb("z_q", [P, S], U32)
+        z_s = sb("z_s", [P, S], U8)
+        for h in range(2):
+            nc.vector.tensor_scalar(
+                z_bf[h][:].rearrange("p (c i) t -> p c t i", i=4),
+                quad[:, :, h * SH : (h + 1) * SH].rearrange("p t (c i) -> p c t i", i=4),
+                0.75, None, MULT,
+            )
+        for h in range(2):
+            cols = slice(h * SH, (h + 1) * SH)
+            nc.vector.quantize_mx(
+                out=z_q[:, cols].bitcast(FP8X4), scales=z_s[:, cols], in_=z_bf[h][:].rearrange("p c t -> p (c t)")
+            )
+        pair = sb("pair", [P, PACK, S], F32)
+        for t in range(PACK):
+            nc.vector.tensor_tensor(pair[:, t, :], y_win[t][:].indirect(n3_l[:]), g4[t][:], ADD)
+
+        a_win = [sb("a_win%d" % b, [P, S], F32) for b in range(4)]
+        a_half = [sb("a_half%d" % b, [P, W], F32) for b in range(4)]
+        for b in range(4):
+            cols = slice(b * P, (b + 1) * P)
+            bank = product("ab%d" % b, cand_w[:, cols], cand_s[:, cols], z_q[:], z_s[:])
+            nc.scalar.activation(a_win[b][:], bank[:], COPY, scale=0.0625)
+            nc.scalar.activation(a_half[b][:], a_win[b][:].indirect(n5_l[:]), COPY, scale=-0.5)
+
+        z2_bf = [sb("z2_bf%d" % h, [P, S // 2, PACK], BF16) for h in range(2)]
+        z2_q = sb("z2_q", [P, S], U32)
+        z2_s = sb("z2_s", [P, S], U8)
+        gk_b = gk4[:].unsqueeze(1).unsqueeze(3).to_broadcast([P, S // 4, PACK, 2])
+        for h in range(2):
+            nc.vector.tensor_tensor(
+                z2_bf[h][:].rearrange("p (c i) t -> p c t i", i=2),
+                pair[:, :, h * (S // 2) : (h + 1) * (S // 2)].rearrange("p t (c i) -> p c t i", i=2),
+                gk_b, MULT,
+            )
+        for h in range(2):
+            cols = slice(h * (S // 2), (h + 1) * (S // 2))
+            nc.vector.quantize_mx(
+                out=z2_q[:, cols].bitcast(FP8X4), scales=z2_s[:, cols], in_=z2_bf[h][:].rearrange("p c t -> p (c t)")
+            )
+
+        b_ps = []
+        for b in range(4):
+            cols = slice(b * P, (b + 1) * P)
+            b_ps.append(product("yb%d" % b, key_w[:, cols], key_s[:, cols], z2_q[:], z2_s[:]))
+        b_win = [sb("b_win%d" % b, [P, S], F32) for b in range(4)]
+        picked = [sb("picked%d" % b, [P, W], F32) for b in range(4)]
+        for b in (0, 2):
+            nc.scalar.activation(b_win[b][:], b_ps[b][:], COPY, scale=0.0625)
+            nc.scalar.activation(picked[b][:], b_win[b][:].indirect(n6_l[:]), COPY)
+        for b in (1, 3):
+            nc.vector.tensor_scalar(b_win[b][:], b_ps[b][:], 0.0625, None, MULT)
+        for b in (1, 3):
+            nc.vector.tensor_tensor(picked[b][:], b_win[b][:].indirect(n6_l[:]), a_half[b][:], ADD)
+        for b in range(4):
+            if b % 2 == 0:
+                nc.vector.tensor_tensor(a_win[b][:].indirect(n5_l[:]), picked[b][:], a_half[b][:], ADD)
+            else:
+                nc.scalar.activation(a_win[b][:].indirect(n5_l[:]), picked[b][:], COPY)
+            nc.sync.dma_start(out[b * P : (b + 1) * P, :], a_win[b][:])

@@ -47,31 +47,36 @@ def tile_picked_cdkeyputbquadsum_none_p_kernel(
         for t in range(PACK):
             nc.vector.memset(y_win[t][:, S:], 0.0)
 
+        yk_win = [sb("yk_win%d" % t, [P, S + 16], F32) for t in range(PACK)]
+        for t in range(PACK):
+            nc.vector.memset(yk_win[t][:, S:], 0.0)
+
         x_tab_w = sb("x_tab_w", [P, T], I32)
         x_scale_rows = x_scales[0].bitcast(I32)
         offs_l = load_list("offs_l", offs)
-        cand_l = load_list("cand_l", cand)
-        for q in range(P // QUAD):
-            rows = x_scale_rows[PACK * q : PACK * (q + 1), :].unsqueeze(0).to_broadcast([QUAD // PACK, PACK, T // 4])
-            nc.scalar.dma_start(x_tab_s[:].bitcast(I32)[QUAD * q : QUAD * (q + 1), :], rows)
         halves = 2
         HW = H // halves
         w_raw = [sb("w_raw%d" % h, [P, PACK, HW], F32) for h in range(halves)]
         w_rows = w1.rearrange("(p j) c -> p j c", j=PACK)
-        for h in range(halves):
-            nc.sync.dma_start(w_raw[h][:], w_rows[:, :, h * HW : (h + 1) * HW])
-            if h == 0:
-                nc.sync.dma_start(x_tab_w[:], x_words[0].rearrange("p n t -> p (n t)").bitcast(I32))
+        nc.scalar.dma_start(w_raw[0][:], w_rows[:, :, :HW])
+        for q in range(P // QUAD):
+            rows = x_scale_rows[PACK * q : PACK * (q + 1), :].unsqueeze(0).to_broadcast([QUAD // PACK, PACK, T // 4])
+            nc.sync.dma_start(x_tab_s[:].bitcast(I32)[QUAD * q : QUAD * (q + 1), :], rows)
+        cand_l = load_list("cand_l", cand)
+        nc.sync.dma_start(x_tab_w[:], x_words[0].rearrange("p n t -> p (n t)").bitcast(I32))
+        nc.sync.dma_start(w_raw[1][:], w_rows[:, :, HW:])
         n1_l = load_list("n1_l", n1)
         n2_l = load_list("n2_l", n2)
+        gs4 = sb("gs4", [P, PACK], F32)
+        gk4 = sb("gk4", [P, PACK], F32)
+        nc.sync.dma_start(gk4[:], gk.rearrange("(p t) o -> p (t o)", t=PACK))
+        nc.sync.dma_start(gs4[:], gs.rearrange("(p t) o -> p (t o)", t=PACK))
         k1_l = load_list("k1_l", k1)
         d_tab_w = sb("d_tab_w", [P, G], I32)
         nc.sync.dma_start(d_tab_w[:], d_words[0].rearrange("p n t -> p (n t)").bitcast(I32))
         nc.sync.dma_start(d_tab_s[:].bitcast(I32)[0:P:8, :], d_scales[0].bitcast(I32))
-        gs4 = sb("gs4", [P, PACK], F32)
-        gk4 = sb("gk4", [P, PACK], F32)
-        nc.sync.dma_start(gs4[:], gs.rearrange("(p t) o -> p (t o)", t=PACK))
-        nc.sync.dma_start(gk4[:], gk.rearrange("(p t) o -> p (t o)", t=PACK))
+        gs75 = sb("gs75", [P, PACK], F32)
+        nc.gpsimd.tensor_scalar(gs75[:], gs4[:], 0.75, 0.0, MULT, ADD)
         n4_l = load_list("n4_l", n4)
         n3_l = load_list("n3_l", n3)
         n5_l = load_list("n5_l", n5)
@@ -98,8 +103,7 @@ def tile_picked_cdkeyputbquadsum_none_p_kernel(
         for h in range(halves):
             src = w_raw[h][:].rearrange("p j (m t) -> p m j t", t=PACK)
             for u in range(2):
-                deal = nc.vector.tensor_copy if (h, u) == (1, 0) else nc.scalar.copy
-                deal(
+                nc.scalar.copy(
                     w_bf[u][:, :, h * MH : (h + 1) * MH, :].rearrange("p e m j -> p m j e"),
                     src[:, :, :, 2 * u : 2 * u + 2],
                 )
@@ -108,8 +112,8 @@ def tile_picked_cdkeyputbquadsum_none_p_kernel(
                 out=w_q[u][:].bitcast(FP8X4), scales=w_s[u][:], in_=w_bf[u][:].rearrange("p e m j -> p (e m j)")
             )
 
-        def product(tag, lhs_w, lhs_s, rhs_w, rhs_s):
-            bank = psum.tile([P, 512], F32, name=tag, tag=tag)
+        def product(tag, lhs_w, lhs_s, rhs_w, rhs_s, width=S):
+            bank = psum.tile([P, width], F32, name=tag, tag=tag)
             nc.tensor.matmul_mx(
                 out=bank[:], lhsT=lhs_w.bitcast(FP8X4), lhsT_scale=lhs_s, rhs=rhs_w.bitcast(FP8X4), rhs_scale=rhs_s,
                 start=True, stop=True,
@@ -128,45 +132,49 @@ def tile_picked_cdkeyputbquadsum_none_p_kernel(
         d1 = [sb("d1_%d" % t, [P, S], F32) for t in range(PACK)]
         d2 = [sb("d2_%d" % t, [P, S], F32) for t in range(PACK)]
         quad = sb("quad", [P, PACK, S], F32)
+        last = PACK - 1
         for t in range(PACK):
             nc.scalar.copy(y_win[t][:, :S], y_ps[t][:])
             nc.scalar.activation(g1[t][:], y_win[t][:].indirect(n1_l[:]), COPY)
-            if t == PACK - 1:
+            if t < last:
                 nc.vector.tensor_copy(g2[t][:], y_win[t][:].indirect(n2_l[:]))
+                nc.gpsimd.tensor_tensor(d2[t][:], g2[t][:], y_win[t][:, :S], SUB)
+                nc.gpsimd.tensor_tensor(d1[t][:], g1[t][:], y_win[t][:, :S], SUB)
             else:
                 nc.scalar.activation(g2[t][:], y_win[t][:].indirect(n2_l[:]), COPY)
-            nc.vector.tensor_tensor(d1[t][:], g1[t][:], y_win[t][:, :S], SUB)
-            nc.vector.tensor_tensor(d2[t][:], g2[t][:], y_win[t][:, :S], SUB)
-            if t == 0:
+                nc.vector.tensor_tensor(d1[t][:], g1[t][:], y_ps[t][:], SUB)
+                nc.vector.tensor_tensor(d2[t][:], g2[t][:], y_ps[t][:], SUB)
+            if t == 1:
                 key_gs = gather_bytes("key_gs", d_tab_s, k1_l)
                 key_w = gather_words("key_w", d_tab_w, k1_l)
                 for r in range(PACK):
                     nc.sync.dma_start(key_s[:].bitcast(I32)[r:P:QUAD, :], key_gs[:].bitcast(I32)[8 * r : P : QUAD, :])
-            nc.vector.scalar_tensor_tensor(quad[:, t, :], d1[t][:], gs4[:, t : t + 1], d2[t][:], MULT, MULT)
+        for t in range(PACK):
+            nc.vector.scalar_tensor_tensor(quad[:, t, :], d1[t][:], gs75[:, t : t + 1], d2[t][:], MULT, MULT)
 
         g4 = [sb("g4_%d" % t, [P, S], F32) for t in range(PACK)]
         for t in range(PACK):
-            nc.scalar.activation(g4[t][:], y_win[t][:].indirect(n4_l[:]), COPY, scale=0.75)
+            if t < 2:
+                nc.gpsimd.tensor_scalar(yk_win[t][:, :S], y_win[t][:, :S], gk4[:, t : t + 1], 0.0, MULT, ADD)
+            else:
+                nc.scalar.activation(yk_win[t][:, :S], y_win[t][:, :S], COPY, scale=gk4[:, t : t + 1])
+        for t in range(PACK):
+            nc.scalar.activation(g4[t][:], yk_win[t][:].indirect(n4_l[:]), COPY, scale=0.75)
 
         SH = S // 2
         z_bf = [sb("z_bf%d" % h, [P, SH, PACK], BF16) for h in range(2)]
         z_q = sb("z_q", [P, S], U32)
         z_s = sb("z_s", [P, S], U8)
         for h in range(2):
-            nc.vector.tensor_scalar(
+            nc.vector.tensor_copy(
                 z_bf[h][:].rearrange("p (c i) t -> p c t i", i=4),
                 quad[:, :, h * SH : (h + 1) * SH].rearrange("p t (c i) -> p c t i", i=4),
-                0.75, None, MULT,
             )
         for h in range(2):
             cols = slice(h * SH, (h + 1) * SH)
             nc.vector.quantize_mx(
                 out=z_q[:, cols].bitcast(FP8X4), scales=z_s[:, cols], in_=z_bf[h][:].rearrange("p c t -> p (c t)")
             )
-        pair = sb("pair", [P, PACK, S], F32)
-        for t in range(PACK):
-            nc.vector.tensor_tensor(pair[:, t, :], y_win[t][:].indirect(n3_l[:]), g4[t][:], ADD)
-
         a_win = [sb("a_win%d" % b, [P, S], F32) for b in range(4)]
         a_half = [sb("a_half%d" % b, [P, W], F32) for b in range(4)]
         for b in range(4):
@@ -175,33 +183,35 @@ def tile_picked_cdkeyputbquadsum_none_p_kernel(
             nc.scalar.activation(a_win[b][:], bank[:], COPY, scale=0.0625)
             nc.scalar.activation(a_half[b][:], a_win[b][:].indirect(n5_l[:]), COPY, scale=-0.5)
 
-        z2_bf = [sb("z2_bf%d" % h, [P, S // 2, PACK], BF16) for h in range(2)]
-        z2_q = sb("z2_q", [P, S], U32)
-        z2_s = sb("z2_s", [P, S], U8)
-        gk_b = gk4[:].unsqueeze(1).unsqueeze(3).to_broadcast([P, S // 4, PACK, 2])
-        for h in range(2):
-            nc.vector.tensor_tensor(
-                z2_bf[h][:].rearrange("p (c i) t -> p c t i", i=2),
-                pair[:, :, h * (S // 2) : (h + 1) * (S // 2)].rearrange("p t (c i) -> p c t i", i=2),
-                gk_b, MULT,
-            )
-        for h in range(2):
-            cols = slice(h * (S // 2), (h + 1) * (S // 2))
-            nc.vector.quantize_mx(
-                out=z2_q[:, cols].bitcast(FP8X4), scales=z2_s[:, cols], in_=z2_bf[h][:].rearrange("p c t -> p (c t)")
-            )
-
-        b_ps = []
-        for b in range(4):
-            cols = slice(b * P, (b + 1) * P)
-            b_ps.append(product("yb%d" % b, key_w[:, cols], key_s[:, cols], z2_q[:], z2_s[:]))
+        pair = [sb("pair%d" % h, [P, PACK, SH], F32, "z_bf%d" % (1 - h)) for h in range(2)]
+        z2_bf = [sb("z2_bf%d" % h, [P, SH, PACK], BF16) for h in range(2)]
+        z2_q = [sb("z2_q%d" % h, [P, SH], U32) for h in range(2)]
+        z2_s = [sb("z2_s%d" % h, [P, SH], U8) for h in range(2)]
         b_win = [sb("b_win%d" % b, [P, S], F32) for b in range(4)]
+        for h in range(2):
+            cols = slice(h * SH, (h + 1) * SH)
+            for t in range(PACK):
+                nc.vector.tensor_tensor(
+                    pair[h][:, t, :], yk_win[t][:].indirect(n3_l[:, h * SH // 16 : (h + 1) * SH // 16]), g4[t][:, cols], ADD
+                )
+            nc.vector.tensor_copy(
+                z2_bf[h][:].rearrange("p (c i) t -> p c t i", i=4), pair[h][:].rearrange("p t (c i) -> p c t i", i=4)
+            )
+            nc.vector.quantize_mx(
+                out=z2_q[h][:].bitcast(FP8X4), scales=z2_s[h][:], in_=z2_bf[h][:].rearrange("p c t -> p (c t)")
+            )
+            for b in range(4):
+                keys = slice(b * P, (b + 1) * P)
+                tag = ("yb%d" if h == 0 else "ab%d") % b
+                bank = product(tag, key_w[:, keys], key_s[:, keys], z2_q[h][:], z2_s[h][:], SH)
+                if h == 1 and b % 2 == 1:
+                    nc.vector.tensor_scalar(b_win[b][:, cols], bank[:], 0.0625, None, MULT)
+                else:
+                    nc.scalar.activation(b_win[b][:, cols], bank[:], COPY, scale=0.0625)
+
         picked = [sb("picked%d" % b, [P, W], F32) for b in range(4)]
         for b in (0, 2):
-            nc.scalar.activation(b_win[b][:], b_ps[b][:], COPY, scale=0.0625)
             nc.scalar.activation(picked[b][:], b_win[b][:].indirect(n6_l[:]), COPY)
-        for b in (1, 3):
-            nc.vector.tensor_scalar(b_win[b][:], b_ps[b][:], 0.0625, None, MULT)
         for b in (1, 3):
             nc.vector.tensor_tensor(picked[b][:], b_win[b][:].indirect(n6_l[:]), a_half[b][:], ADD)
         for b in range(4):

from contextlib import ExitStack

import concourse.mybir as mybir

K, T, S, H, C, G, W = 512, 1024, 512, 512, 512, 2048, 256
FLOPS = 3 * 2 * 512 * 512 * 512

F32 = mybir.dt.float32
BF16 = mybir.dt.bfloat16
I32 = mybir.dt.int32
U32 = mybir.dt.uint32
U16 = mybir.dt.uint16
U8 = mybir.dt.uint8
FP8X4 = mybir.dt.float8_e4m3fn_x4
MULT = mybir.AluOpType.mult
ADD = mybir.AluOpType.add
SUB = mybir.AluOpType.subtract
COPY = mybir.ActivationFunctionType.Copy

P = 128
PACK = 4
QUAD = 32


def tile_picked_cdkeyputbquadsum_none_p_kernel(
    tc, x_words, x_scales, w1, gs, gk, d_words, d_scales, offs, n1, n2, n3, n4, cand, k1, n5, n6, out
):
    nc = tc.nc
    with ExitStack() as ctx:
        keep = ctx.enter_context(tc.tile_pool(name="keep", bufs=1))
        psum = ctx.enter_context(tc.psum_pool(name="psum", bufs=1))

        def sb(name, shape, dtype, tag=None):
            return keep.tile(shape, dtype, name=name, tag=tag or name, align_bytes=64)

        def load_list(name, src):
            tile = sb(name, list(src.shape), U16)
            nc.sync.dma_start(tile[:], src)
            return tile

        x_tab_s = sb("x_tab_s", [P, T], U8)
        d_tab_s = sb("d_tab_s", [P, G], U8)
        key_s = sb("key_s", [P, H], U8)
        nc.vector.memset(d_tab_s[:].bitcast(I32), 0)
        nc.vector.memset(key_s[:].bitcast(I32), 0)
        y_win = [sb("y_win%d" % t, [P, 2 * S], F32) for t in range(PACK)]
        for t in range(PACK):
            nc.vector.memset(y_win[t][:, S:], 0.0)

        yk_win = [sb("yk_win%d" % t, [P, S + 16], F32) for t in range(PACK)]
        for t in range(PACK):
            nc.vector.memset(yk_win[t][:, S:], 0.0)

        x_tab_w = sb("x_tab_w", [P, T], I32)
        x_scale_rows = x_scales[0].bitcast(I32)
        offs_l = load_list("offs_l", offs)
        halves = 2
        HW = H // halves
        w_raw = [sb("w_raw%d" % h, [P, PACK, HW], F32) for h in range(halves)]
        w_rows = w1.rearrange("(p j) c -> p j c", j=PACK)
        nc.scalar.dma_start(w_raw[0][:], w_rows[:, :, :HW])
        for q in range(P // QUAD):
            rows = x_scale_rows[PACK * q : PACK * (q + 1), :].unsqueeze(0).to_broadcast([QUAD // PACK, PACK, T // 4])
            nc.sync.dma_start(x_tab_s[:].bitcast(I32)[QUAD * q : QUAD * (q + 1), :], rows)
        cand_l = load_list("cand_l", cand)
        nc.sync.dma_start(x_tab_w[:], x_words[0].rearrange("p n t -> p (n t)").bitcast(I32))
        nc.sync.dma_start(w_raw[1][:], w_rows[:, :, HW:])
        n1_l = load_list("n1_l", n1)
        n2_l = load_list("n2_l", n2)
        gs4 = sb("gs4", [P, PACK], F32)
        gk4 = sb("gk4", [P, PACK], F32)
        nc.sync.dma_start(gk4[:], gk.rearrange("(p t) o -> p (t o)", t=PACK))
        nc.sync.dma_start(gs4[:], gs.rearrange("(p t) o -> p (t o)", t=PACK))
        k1_l = load_list("k1_l", k1)
        d_tab_w = sb("d_tab_w", [P, G], I32)
        nc.sync.dma_start(d_tab_w[:], d_words[0].rearrange("p n t -> p (n t)").bitcast(I32))
        nc.sync.dma_start(d_tab_s[:].bitcast(I32)[0:P:8, :], d_scales[0].bitcast(I32))
        gs75 = sb("gs75", [P, PACK], F32)
        nc.gpsimd.tensor_scalar(gs75[:], gs4[:], 0.75, 0.0, MULT, ADD)
        n4_l = load_list("n4_l", n4)
        n3_l = load_list("n3_l", n3)
        n5_l = load_list("n5_l", n5)
        n6_l = load_list("n6_l", n6)

        def gather_words(name, table, lst, tag=None):
            words = sb(name, [P, 512], U32, tag)
            nc.vector.tensor_copy(words[:], table[:].bitcast(U32).indirect(lst[:]))
            return words

        def gather_bytes(name, table, lst, tag=None):
            scales = sb(name, [P, 512], U8, tag)
            nc.vector.tensor_copy(scales[:], table[:].indirect(lst[:]))
            return scales

        tok_s = gather_bytes("tok_s", x_tab_s, offs_l)
        cand_s = gather_bytes("cand_s", x_tab_s, cand_l)
        tok_w = gather_words("tok_w", x_tab_w, offs_l)

        MH = P // halves
        w_bf = [sb("w_bf%d" % u, [P, 2, P, PACK], BF16) for u in range(2)]
        w_q = [sb("w_q%d" % u, [P, 2 * P], U32) for u in range(2)]
        w_s = [sb("w_s%d" % u, [P, 2 * P], U8) for u in range(2)]
        for h in range(halves):
            src = w_raw[h][:].rearrange("p j (m t) -> p m j t", t=PACK)
            for u in range(2):
                nc.scalar.copy(
                    w_bf[u][:, :, h * MH : (h + 1) * MH, :].rearrange("p e m j -> p m j e"),
                    src[:, :, :, 2 * u : 2 * u + 2],
                )
        for u in range(2):
            nc.vector.quantize_mx(
                out=w_q[u][:].bitcast(FP8X4), scales=w_s[u][:], in_=w_bf[u][:].rearrange("p e m j -> p (e m j)")
            )

        def product(tag, lhs_w, lhs_s, rhs_w, rhs_s, width=S):
            bank = psum.tile([P, width], F32, name=tag, tag=tag)
            nc.tensor.matmul_mx(
                out=bank[:], lhsT=lhs_w.bitcast(FP8X4), lhsT_scale=lhs_s, rhs=rhs_w.bitcast(FP8X4), rhs_scale=rhs_s,
                start=True, stop=True,
            )
            return bank

        y_ps = []
        for t in range(PACK):
            cols = slice((t % 2) * P, (t % 2 + 1) * P)
            y_ps.append(product("yb%d" % t, w_q[t // 2][:, cols], w_s[t // 2][:, cols], tok_w[:], tok_s[:]))

        cand_w = gather_words("cand_w", x_tab_w, cand_l, "w_bf1")

        g1 = [sb("g1_%d" % t, [P, S], F32) for t in range(PACK)]
        g2 = [sb("g2_%d" % t, [P, S], F32) for t in range(PACK)]
        d1 = [sb("d1_%d" % t, [P, S], F32) for t in range(PACK)]
        d2 = [sb("d2_%d" % t, [P, S], F32) for t in range(PACK)]
        quad = sb("quad", [P, PACK, S], F32)
        last = PACK - 1
        for t in range(PACK):
            nc.scalar.copy(y_win[t][:, :S], y_ps[t][:])
            nc.scalar.activation(g1[t][:], y_win[t][:].indirect(n1_l[:]), COPY)
            if t < last:
                nc.vector.tensor_copy(g2[t][:], y_win[t][:].indirect(n2_l[:]))
                nc.gpsimd.tensor_tensor(d2[t][:], g2[t][:], y_win[t][:, :S], SUB)
                nc.gpsimd.tensor_tensor(d1[t][:], g1[t][:], y_win[t][:, :S], SUB)
            else:
                nc.scalar.activation(g2[t][:], y_win[t][:].indirect(n2_l[:]), COPY)
                nc.vector.tensor_tensor(d1[t][:], g1[t][:], y_ps[t][:], SUB)
                nc.vector.tensor_tensor(d2[t][:], g2[t][:], y_ps[t][:], SUB)
            if t == 1:
                key_gs = gather_bytes("key_gs", d_tab_s, k1_l)
                key_w = gather_words("key_w", d_tab_w, k1_l)
                for r in range(PACK):
                    nc.sync.dma_start(key_s[:].bitcast(I32)[r:P:QUAD, :], key_gs[:].bitcast(I32)[8 * r : P : QUAD, :])
        for t in range(PACK):
            nc.vector.scalar_tensor_tensor(quad[:, t, :], d1[t][:], gs75[:, t : t + 1], d2[t][:], MULT, MULT)

        g4 = [sb("g4_%d" % t, [P, S], F32) for t in range(PACK)]
        for t in range(PACK):
            if t < 2:
                nc.gpsimd.tensor_scalar(yk_win[t][:, :S], y_win[t][:, :S], gk4[:, t : t + 1], 0.0, MULT, ADD)
            else:
                nc.scalar.activation(yk_win[t][:, :S], y_win[t][:, :S], COPY, scale=gk4[:, t : t + 1])
        for t in range(PACK):
            nc.scalar.activation(g4[t][:], yk_win[t][:].indirect(n4_l[:]), COPY, scale=0.75)

        SH = S // 2
        z_bf = [sb("z_bf%d" % h, [P, SH, PACK], BF16) for h in range(2)]
        z_q = sb("z_q", [P, S], U32)
        z_s = sb("z_s", [P, S], U8)
        for h in range(2):
            nc.vector.tensor_copy(
                z_bf[h][:].rearrange("p (c i) t -> p c t i", i=4),
                quad[:, :, h * SH : (h + 1) * SH].rearrange("p t (c i) -> p c t i", i=4),
            )
        for h in range(2):
            cols = slice(h * SH, (h + 1) * SH)
            nc.vector.quantize_mx(
                out=z_q[:, cols].bitcast(FP8X4), scales=z_s[:, cols], in_=z_bf[h][:].rearrange("p c t -> p (c t)")
            )
        a_win = [sb("a_win%d" % b, [P, S], F32) for b in range(4)]
        a_half = [sb("a_half%d" % b, [P, W], F32) for b in range(4)]
        for b in range(4):
            cols = slice(b * P, (b + 1) * P)
            bank = product("ab%d" % b, cand_w[:, cols], cand_s[:, cols], z_q[:], z_s[:])
            nc.scalar.activation(a_win[b][:], bank[:], COPY, scale=0.0625)
            nc.scalar.activation(a_half[b][:], a_win[b][:].indirect(n5_l[:]), COPY, scale=-0.5)

        pair = [sb("pair%d" % h, [P, PACK, SH], F32, "z_bf%d" % (1 - h)) for h in range(2)]
        z2_bf = [sb("z2_bf%d" % h, [P, SH, PACK], BF16) for h in range(2)]
        z2_q = [sb("z2_q%d" % h, [P, SH], U32) for h in range(2)]
        z2_s = [sb("z2_s%d" % h, [P, SH], U8) for h in range(2)]
        b_win = [sb("b_win%d" % b, [P, S], F32) for b in range(4)]
        for h in range(2):
            cols = slice(h * SH, (h + 1) * SH)
            for t in range(PACK):
                nc.vector.tensor_tensor(
                    pair[h][:, t, :], yk_win[t][:].indirect(n3_l[:, h * SH // 16 : (h + 1) * SH // 16]), g4[t][:, cols], ADD
                )
            nc.vector.tensor_copy(
                z2_bf[h][:].rearrange("p (c i) t -> p c t i", i=4), pair[h][:].rearrange("p t (c i) -> p c t i", i=4)
            )
            nc.vector.quantize_mx(
                out=z2_q[h][:].bitcast(FP8X4), scales=z2_s[h][:], in_=z2_bf[h][:].rearrange("p c t -> p (c t)")
            )
            for b in range(4):
                keys = slice(b * P, (b + 1) * P)
                tag = ("yb%d" if h == 0 else "ab%d") % b
                bank = product(tag, key_w[:, keys], key_s[:, keys], z2_q[h][:], z2_s[h][:], SH)
                if h == 1 and b % 2 == 1:
                    nc.vector.tensor_scalar(b_win[b][:, cols], bank[:], 0.0625, None, MULT)
                else:
                    nc.scalar.activation(b_win[b][:, cols], bank[:], COPY, scale=0.0625)

        picked = [sb("picked%d" % b, [P, W], F32) for b in range(4)]
        for b in (0, 2):
            nc.scalar.activation(picked[b][:], b_win[b][:].indirect(n6_l[:]), COPY)
        for b in (1, 3):
            nc.vector.tensor_tensor(picked[b][:], b_win[b][:].indirect(n6_l[:]), a_half[b][:], ADD)
        for b in range(4):
            if b % 2 == 0:
                nc.vector.tensor_tensor(a_win[b][:].indirect(n5_l[:]), picked[b][:], a_half[b][:], ADD)
            else:
                nc.scalar.activation(a_win[b][:].indirect(n5_l[:]), picked[b][:], COPY)
            nc.sync.dma_start(out[b * P : (b + 1) * P, :], a_win[b][:])
